import numpy as np
import ml_dtypes

BF16 = ml_dtypes.bfloat16


def bf(x):
    return np.asarray(x, np.float32).astype(BF16)


def f32(x):
    return np.asarray(x, np.float32)


def f64(x):
    return np.asarray(x).astype(np.float64)


def striped(idx):
    return np.tile(idx.reshape(-1, 16).T, (8, 1))


S, K, M, N, D, V = 256, 128, 128, 256, 4, 64


def setup_inputs():
    return {"table": bf(np.random.standard_normal((S, K))), "w": bf(np.random.standard_normal((K, M)) / np.sqrt(D * K)), "b": f32(0.5 * np.random.standard_normal((M, 1))), "offs": striped(np.random.permutation(np.tile(np.arange(S), 2))[:N])}


def reference(table, w, b, offs):
    idx = offs[:16].T.reshape(-1)
    x = f64(table)[idx].T
    y = f64(w).T @ sum(x[:, t * V : (t + 1) * V] for t in range(D))
    return np.tanh(y + f64(b))

@@ -1,0 +1,59 @@
+import concourse.mybir as mybir
+from concourse.masks import make_identity
+
+P = 128
+NODES = 256
+FEATURES = 128
+OUT_FEATURES = 128
+NEIGHBOURS = 4
+PIECE = 64
+LIST = NEIGHBOURS * PIECE
+PIECE_COLUMNS = PIECE // 16
+NODE_BLOCKS = NODES // P
+
+FLOPS = (NEIGHBOURS - 1) * FEATURES * PIECE + 2 * FEATURES * OUT_FEATURES * PIECE
+
+BF16 = mybir.dt.bfloat16
+F32 = mybir.dt.float32
+U16 = mybir.dt.uint16
+
+
+def tile_gather_matmul_kernel(tc, table, w, b, offs, out):
+    nc = tc.nc
+    with (
+        tc.tile_pool(name="held", bufs=1) as held,
+        tc.psum_pool(name="psum", bufs=1) as psum,
+    ):
+        offsets = held.tile([P, LIST // 16], U16, name="offsets")
+        nc.sync.dma_start(offsets[:], offs)
+        node_rows = held.tile([P, NODE_BLOCKS, FEATURES], BF16, name="node_rows")
+        nc.scalar.dma_start(node_rows[:], table.rearrange("(a p) k -> p a k", p=P))
+        weights = held.tile([FEATURES, OUT_FEATURES], BF16, name="weights")
+        nc.sync.dma_start(weights[:], w)
+        bias = held.tile([OUT_FEATURES, 1], F32, name="bias")
+        nc.scalar.dma_start(bias[:], b)
+
+        identity = held.tile([P, P], BF16, name="identity")
+        make_identity(nc, identity[:])
+        flipped = psum.tile([FEATURES, NODES], BF16, name="flipped")
+        for a in range(NODE_BLOCKS):
+            nc.tensor.transpose(flipped[:, a * P : (a + 1) * P], node_rows[:, a, :], identity[:])
+        window = held.tile([FEATURES, NODES], BF16, name="window")
+        nc.vector.tensor_copy(window[:], flipped[:])
+
+        summed = psum.tile([OUT_FEATURES, PIECE], F32, name="summed")
+        for t in range(NEIGHBOURS):
+            piece = offsets[:, t * PIECE_COLUMNS : (t + 1) * PIECE_COLUMNS]
+            nc.tensor.matmul(
+                summed[:],
+                weights[:],
+                window[:].indirect(piece),
+                start=(t == 0),
+                stop=(t == NEIGHBOURS - 1),
+            )
+
+        result = held.tile([OUT_FEATURES, PIECE], F32, name="result")
+        nc.scalar.activation(
+            result[:], summed[:], mybir.ActivationFunctionType.Tanh, bias=bias[:, 0:1]
+        )
+        nc.sync.dma_start(out, result[:])

@@ -33,6 +33,10 @@ def tile_gather_matmul_kernel(tc, table, w, b, offs, out):
         bias = held.tile([OUT_FEATURES, 1], F32, name="bias")
         nc.scalar.dma_start(bias[:], b)
 
+        warm = held.tile([P, 1], F32, name="warm")
+        nc.vector.memset(warm[:], 0.0)
+        nc.scalar.activation(warm[:], warm[:], mybir.ActivationFunctionType.Tanh)
+
         identity = held.tile([P, P], BF16, name="identity")
         make_identity(nc, identity[:])
         flipped = psum.tile([FEATURES, NODES], BF16, name="flipped")

@@ -10,6 +10,7 @@ PIECE = 64
 LIST = NEIGHBOURS * PIECE
 PIECE_COLUMNS = PIECE // 16
 NODE_BLOCKS = NODES // P
+WARM_UPS = 16
 
 FLOPS = (NEIGHBOURS - 1) * FEATURES * PIECE + 2 * FEATURES * OUT_FEATURES * PIECE
 
@@ -33,9 +34,11 @@ def tile_gather_matmul_kernel(tc, table, w, b, offs, out):
         bias = held.tile([OUT_FEATURES, 1], F32, name="bias")
         nc.scalar.dma_start(bias[:], b)
 
-        warm = held.tile([P, 1], F32, name="warm")
-        nc.vector.memset(warm[:], 0.0)
-        nc.scalar.activation(warm[:], warm[:], mybir.ActivationFunctionType.Tanh)
+        zeros = held.tile([P, P], BF16, name="zeros")
+        nc.vector.memset(zeros[:], 0.0)
+        unused = psum.tile([P, P], F32, name="unused")
+        for i in range(WARM_UPS):
+            nc.tensor.matmul(unused[:], zeros[:], zeros[:], start=True, stop=True)
 
         identity = held.tile([P, P], BF16, name="identity")
         make_identity(nc, identity[:])

@@ -10,7 +10,6 @@ PIECE = 64
 LIST = NEIGHBOURS * PIECE
 PIECE_COLUMNS = PIECE // 16
 NODE_BLOCKS = NODES // P
-WARM_UPS = 16
 
 FLOPS = (NEIGHBOURS - 1) * FEATURES * PIECE + 2 * FEATURES * OUT_FEATURES * PIECE
 
@@ -25,20 +24,14 @@ def tile_gather_matmul_kernel(tc, table, w, b, offs, out):
         tc.tile_pool(name="held", bufs=1) as held,
         tc.psum_pool(name="psum", bufs=1) as psum,
     ):
+        node_rows = held.tile([P, NODE_BLOCKS, FEATURES], BF16, name="node_rows")
+        nc.sync.dma_start(node_rows[:], table.rearrange("(a p) k -> p a k", p=P))
         offsets = held.tile([P, LIST // 16], U16, name="offsets")
         nc.sync.dma_start(offsets[:], offs)
-        node_rows = held.tile([P, NODE_BLOCKS, FEATURES], BF16, name="node_rows")
-        nc.scalar.dma_start(node_rows[:], table.rearrange("(a p) k -> p a k", p=P))
         weights = held.tile([FEATURES, OUT_FEATURES], BF16, name="weights")
         nc.sync.dma_start(weights[:], w)
         bias = held.tile([OUT_FEATURES, 1], F32, name="bias")
-        nc.scalar.dma_start(bias[:], b)
-
-        zeros = held.tile([P, P], BF16, name="zeros")
-        nc.vector.memset(zeros[:], 0.0)
-        unused = psum.tile([P, P], F32, name="unused")
-        for i in range(WARM_UPS):
-            nc.tensor.matmul(unused[:], zeros[:], zeros[:], start=True, stop=True)
+        nc.sync.dma_start(bias[:], b)
 
         identity = held.tile([P, P], BF16, name="identity")
         make_identity(nc, identity[:])

@@ -22,10 +22,12 @@ def tile_gather_matmul_kernel(tc, table, w, b, offs, out):
     nc = tc.nc
     with (
         tc.tile_pool(name="held", bufs=1) as held,
+        tc.psum_pool(name="flips", bufs=NODE_BLOCKS) as flips,
         tc.psum_pool(name="psum", bufs=1) as psum,
     ):
-        node_rows = held.tile([P, NODE_BLOCKS, FEATURES], BF16, name="node_rows")
-        nc.sync.dma_start(node_rows[:], table.rearrange("(a p) k -> p a k", p=P))
+        node_rows = [held.tile([P, FEATURES], BF16, name="node_rows%d" % a) for a in range(NODE_BLOCKS)]
+        nc.sync.dma_start(node_rows[0][:], table[0:P, :])
+        nc.scalar.dma_start(node_rows[1][:], table[P : 2 * P, :])
         offsets = held.tile([P, LIST // 16], U16, name="offsets")
         nc.sync.dma_start(offsets[:], offs)
         weights = held.tile([FEATURES, OUT_FEATURES], BF16, name="weights")
@@ -33,13 +35,17 @@ def tile_gather_matmul_kernel(tc, table, w, b, offs, out):
         bias = held.tile([OUT_FEATURES, 1], F32, name="bias")
         nc.sync.dma_start(bias[:], b)
 
+        warm = held.tile([P, 1], F32, name="warm")
+        nc.vector.memset(warm[:], 0.0)
+        nc.scalar.activation(warm[:], warm[:], mybir.ActivationFunctionType.Tanh)
+
         identity = held.tile([P, P], BF16, name="identity")
         make_identity(nc, identity[:])
-        flipped = psum.tile([FEATURES, NODES], BF16, name="flipped")
-        for a in range(NODE_BLOCKS):
-            nc.tensor.transpose(flipped[:, a * P : (a + 1) * P], node_rows[:, a, :], identity[:])
         window = held.tile([FEATURES, NODES], BF16, name="window")
-        nc.vector.tensor_copy(window[:], flipped[:])
+        for a in range(NODE_BLOCKS):
+            flipped = flips.tile([FEATURES, P], BF16, name="flipped")
+            nc.tensor.transpose(flipped[:], node_rows[a][:], identity[:])
+            nc.vector.tensor_copy(window[:, a * P : (a + 1) * P], flipped[:])
 
         summed = psum.tile([OUT_FEATURES, PIECE], F32, name="summed")
         for t in range(NEIGHBOURS):

@@ -62,4 +62,4 @@ def tile_gather_matmul_kernel(tc, table, w, b, offs, out):
         nc.scalar.activation(
             result[:], summed[:], mybir.ActivationFunctionType.Tanh, bias=bias[:, 0:1]
         )
-        nc.sync.dma_start(out, result[:])
+        nc.scalar.dma_start(out, result[:])

@@ -40,7 +40,8 @@ def tile_gather_matmul_kernel(tc, table, w, b, offs, out):
         nc.scalar.activation(warm[:], warm[:], mybir.ActivationFunctionType.Tanh)
 
         identity = held.tile([P, P], BF16, name="identity")
-        make_identity(nc, identity[:])
+        nc.vector.memset(identity[:], 0.0)
+        make_identity(nc, identity[:], nomemset=True)
         window = held.tile([FEATURES, NODES], BF16, name="window")
         for a in range(NODE_BLOCKS):
             flipped = flips.tile([FEATURES, P], BF16, name="flipped")

@@ -10,6 +10,8 @@ PIECE = 64
 LIST = NEIGHBOURS * PIECE
 PIECE_COLUMNS = PIECE // 16
 NODE_BLOCKS = NODES // P
+WARM_REPEATS = 4
+WARM_MATMULS = 3
 
 FLOPS = (NEIGHBOURS - 1) * FEATURES * PIECE + 2 * FEATURES * OUT_FEATURES * PIECE
 
@@ -25,6 +27,18 @@ def tile_gather_matmul_kernel(tc, table, w, b, offs, out):
         tc.psum_pool(name="flips", bufs=NODE_BLOCKS) as flips,
         tc.psum_pool(name="psum", bufs=1) as psum,
     ):
+        zeros = held.tile([P, P], BF16, name="zeros")
+        nc.vector.memset(zeros[:], 0.0)
+        idle_product = psum.tile([P, WARM_REPEATS, P], F32, name="idle_product")
+        for i in range(WARM_MATMULS):
+            nc.tensor.matmul(
+                idle_product[:],
+                zeros[:],
+                zeros[:].unsqueeze(1).to_broadcast([P, WARM_REPEATS, P]),
+                start=True,
+                stop=True,
+            )
+
         node_rows = [held.tile([P, FEATURES], BF16, name="node_rows%d" % a) for a in range(NODE_BLOCKS)]
         nc.sync.dma_start(node_rows[0][:], table[0:P, :])
         nc.scalar.dma_start(node_rows[1][:], table[P : 2 * P, :])

@@ -27,14 +27,14 @@ def tile_gather_matmul_kernel(tc, table, w, b, offs, out):
         tc.psum_pool(name="flips", bufs=NODE_BLOCKS) as flips,
         tc.psum_pool(name="psum", bufs=1) as psum,
     ):
-        zeros = held.tile([P, P], BF16, name="zeros")
-        nc.vector.memset(zeros[:], 0.0)
-        idle_product = psum.tile([P, WARM_REPEATS, P], F32, name="idle_product")
+        zeros = held.tile([P, 2], BF16, name="zeros")
+        nc.gpsimd.memset(zeros[:], 0.0)
+        idle_product = psum.tile([P, WARM_REPEATS * P], F32, name="idle_product")
         for i in range(WARM_MATMULS):
             nc.tensor.matmul(
                 idle_product[:],
-                zeros[:],
-                zeros[:].unsqueeze(1).to_broadcast([P, WARM_REPEATS, P]),
+                zeros[:, 0:1].to_broadcast([P, P]),
+                zeros[:, 0:1].to_broadcast([P, WARM_REPEATS * P]),
                 start=True,
                 stop=True,
             )

import concourse.mybir as mybir
from concourse.masks import make_identity

P = 128
NODES = 256
FEATURES = 128
OUT_FEATURES = 128
NEIGHBOURS = 4
PIECE = 64
LIST = NEIGHBOURS * PIECE
PIECE_COLUMNS = PIECE // 16
NODE_BLOCKS = NODES // P
WARM_REPEATS = 4
WARM_MATMULS = 3

FLOPS = (NEIGHBOURS - 1) * FEATURES * PIECE + 2 * FEATURES * OUT_FEATURES * PIECE

BF16 = mybir.dt.bfloat16
F32 = mybir.dt.float32
U16 = mybir.dt.uint16


def tile_gather_matmul_kernel(tc, table, w, b, offs, out):
    nc = tc.nc
    with (
        tc.tile_pool(name="held", bufs=1) as held,
        tc.psum_pool(name="flips", bufs=NODE_BLOCKS) as flips,
        tc.psum_pool(name="psum", bufs=1) as psum,
    ):
        zeros = held.tile([P, 2], BF16, name="zeros")
        nc.gpsimd.memset(zeros[:], 0.0)
        idle_product = psum.tile([P, WARM_REPEATS * P], F32, name="idle_product")
        for i in range(WARM_MATMULS):
            nc.tensor.matmul(
                idle_product[:],
                zeros[:, 0:1].to_broadcast([P, P]),
                zeros[:, 0:1].to_broadcast([P, WARM_REPEATS * P]),
                start=True,
                stop=True,
            )

        node_rows = [held.tile([P, FEATURES], BF16, name="node_rows%d" % a) for a in range(NODE_BLOCKS)]
        nc.sync.dma_start(node_rows[0][:], table[0:P, :])
        nc.scalar.dma_start(node_rows[1][:], table[P : 2 * P, :])
        offsets = held.tile([P, LIST // 16], U16, name="offsets")
        nc.sync.dma_start(offsets[:], offs)
        weights = held.tile([FEATURES, OUT_FEATURES], BF16, name="weights")
        nc.sync.dma_start(weights[:], w)
        bias = held.tile([OUT_FEATURES, 1], F32, name="bias")
        nc.sync.dma_start(bias[:], b)

        warm = held.tile([P, 1], F32, name="warm")
        nc.vector.memset(warm[:], 0.0)
        nc.scalar.activation(warm[:], warm[:], mybir.ActivationFunctionType.Tanh)

        identity = held.tile([P, P], BF16, name="identity")
        nc.vector.memset(identity[:], 0.0)
        make_identity(nc, identity[:], nomemset=True)
        window = held.tile([FEATURES, NODES], BF16, name="window")
        for a in range(NODE_BLOCKS):
            flipped = flips.tile([FEATURES, P], BF16, name="flipped")
            nc.tensor.transpose(flipped[:], node_rows[a][:], identity[:])
            nc.vector.tensor_copy(window[:, a * P : (a + 1) * P], flipped[:])

        summed = psum.tile([OUT_FEATURES, PIECE], F32, name="summed")
        for t in range(NEIGHBOURS):
            piece = offsets[:, t * PIECE_COLUMNS : (t + 1) * PIECE_COLUMNS]
            nc.tensor.matmul(
                summed[:],
                weights[:],
                window[:].indirect(piece),
                start=(t == 0),
                stop=(t == NEIGHBOURS - 1),
            )

        result = held.tile([OUT_FEATURES, PIECE], F32, name="result")
        nc.scalar.activation(
            result[:], summed[:], mybir.ActivationFunctionType.Tanh, bias=bias[:, 0:1]
        )
        nc.scalar.dma_start(out, result[:])
